import numpy as np
import ml_dtypes


def mxq(x, axis, fmt="e4m3"):
    dtype, down = {"e4m3": (ml_dtypes.float8_e4m3fn, 7), "e5m2": (ml_dtypes.float8_e5m2, 14)}[fmt]
    v = np.moveaxis(np.asarray(x, np.float32).astype(ml_dtypes.bfloat16).astype(np.float64), axis, -1)
    blocks = v.reshape(v.shape[:-1] + (-1, 32))
    amax = np.abs(blocks).max(-1, keepdims=True)
    byte = np.maximum(np.where(amax > 0, np.frexp(amax)[1] - 1 + 127, 0) - down, 1)
    scale = np.exp2(byte - 127.0)
    codes = (blocks / scale).astype(np.float32).astype(dtype).astype(np.float64)
    return np.moveaxis((codes * scale).reshape(v.shape), -1, axis)


WIDE = False


def mx_kscale(k):
    if not WIDE:
        return np.ones(k)
    levels = np.array([30, -30])
    if k % 512:
        return np.exp2(np.random.permutation(np.resize(levels, k // 32))).repeat(32)
    a = np.empty((k // 512, 16))
    for p in range(k // 512):
        a[p, :8] = np.random.permutation(np.resize(levels, 8))
        for g in range(8):
            far = levels[np.abs(levels - a[p, g]) >= 10]
            a[p, g + 8] = far[np.random.randint(len(far))]
    return np.exp2(a.ravel()).repeat(32)


def f64(x):
    return np.asarray(x).astype(np.float64)


def striped(idx):
    return np.tile(np.asarray(idx).reshape(-1, 16).T, (8, 1)).astype(np.uint16)


def unstriped(offs):
    return offs[:16].T.reshape(-1).astype(np.int64)


E2M1 = np.array([0.0, 0.5, 1.0, 1.5, 2.0, 3.0, 4.0, 6.0, -0.0, -0.5, -1.0, -1.5, -2.0, -3.0, -4.0, -6.0])


def pack_weight(w, fmt):
    k, n = w.shape
    w = f64(np.asarray(w, np.float32).astype(ml_dtypes.bfloat16)).reshape(k // 32, 32, n)
    amax = np.abs(w).max(1)
    if fmt in ("e4m3", "e5m2"):
        byte = np.frexp(amax)[1] - 1 + 127 - (7 if fmt == "e4m3" else 14)
    else:
        mant, ex = np.frexp(amax / 6.0)
        byte = np.where(mant > 0.5, ex, ex - 1) + 127
    byte = np.clip(np.where(amax > 0, byte, 1), 1, 254)
    scaled = (w * np.exp2(127.0 - byte)[:, None, :]).reshape(k, n).astype(np.float32)
    by_word = np.ascontiguousarray(scaled.reshape(k // 512, 128, 4, n).transpose(0, 1, 3, 2))
    if fmt in ("e4m3", "e5m2"):
        words = by_word.astype(ml_dtypes.float8_e4m3fn if fmt == "e4m3" else ml_dtypes.float8_e5m2).view(np.uint8)
    else:
        c = by_word.astype(ml_dtypes.float4_e2m1fn).view(np.uint8) & 0xF
        words = (c[..., 0::2] | (c[..., 1::2] << 4)).reshape(k // 512, 128, 2 * n)
    return np.ascontiguousarray(words), np.ascontiguousarray(byte.astype(np.uint8).reshape(k // 512, 16, n))


def unpack_weight(words, scales, fmt):
    g, _, n = scales.shape
    words = np.ascontiguousarray(words).reshape(g, 128, n, -1)
    if fmt in ("e4m3", "e5m2"):
        vals = words.view(ml_dtypes.float8_e4m3fn if fmt == "e4m3" else ml_dtypes.float8_e5m2).astype(np.float64)
    else:
        nib = np.empty((g, 128, n, 4), np.uint8)
        nib[..., 0::2] = words & 0xF
        nib[..., 1::2] = words >> 4
        vals = E2M1[nib]
    vals = vals * np.repeat(np.exp2(scales.astype(np.float64) - 127.0), 8, axis=1)[..., None]
    return vals.transpose(0, 1, 3, 2).reshape(g * 512, n)


K, T, J, R, N = 512, 2048, 256, 512, 256


def setup_inputs():
    n = np.random.standard_normal
    idx = np.random.permutation(T)[:J]
    idx2 = np.random.permutation(T)[:J]
    idx3 = np.random.permutation(J)[:J]
    idx4 = np.random.permutation(J)[:J]
    fk = mx_kscale(K)
    fr = mx_kscale(R)
    xtp = pack_weight(n((K, T)) / fk[:, None], "e5m2")
    wp = pack_weight(n((K, R)) * 1 / np.sqrt(K) * fk[:, None] * fr, "e2m1")
    w2p = pack_weight(n((K, R)) * 1 / np.sqrt(K) * fk[:, None] * fr, "e4m3")
    wbp = pack_weight(n((R, N)) * 1 / np.sqrt(R) / fr[:, None], "e2m1")
    wsp = pack_weight(n((K, N)) * 1 / np.sqrt(K) * fk[:, None], "e2m1")
    return {
        "xt_words": xtp[0],
        "xt_scales": xtp[1],
        "w_words": wp[0],
        "w_scales": wp[1],
        "w2_words": w2p[0],
        "w2_scales": w2p[1],
        "wb_words": wbp[0],
        "wb_scales": wbp[1],
        "ws_words": wsp[0],
        "ws_scales": wsp[1],
        "offs": striped(idx),
        "offs2": striped(idx2),
        "offs3": striped(idx3),
        "offs4": striped(idx4),
    }


def reference(xt_words, xt_scales, w_words, w_scales, w2_words, w2_scales, wb_words, wb_scales, ws_words, ws_scales, offs, offs2, offs3, offs4):
    idx = unstriped(offs)
    idx2 = unstriped(offs2)
    idx3 = unstriped(offs3)
    idx4 = unstriped(offs4)
    xtu = unpack_weight(xt_words, xt_scales, "e5m2")
    wu = unpack_weight(w_words, w_scales, "e2m1")
    w2u = unpack_weight(w2_words, w2_scales, "e4m3")
    wbu = unpack_weight(wb_words, wb_scales, "e2m1")
    wsu = unpack_weight(ws_words, ws_scales, "e2m1")
    xtidxg = xtu[:, idx]
    a = wu.T @ xtidxg
    xtidx2g = xtu[:, idx2]
    b = w2u.T @ xtidx2g
    hid = np.maximum(a - b[:, idx3], b - a[:, idx4])
    hidq = mxq(hid, 0, "e4m3")
    y = wbu.T @ hidq + wsu.T @ xtidxg
    return y

from contextlib import ExitStack

import concourse.mybir as mybir

K, T, J, R, N = 512, 2048, 256, 512, 256
FLOPS = 2 * K * J * (2 * R + N) + 2 * R * J * N

F32 = mybir.dt.float32
BF16 = mybir.dt.bfloat16
I32 = mybir.dt.int32
U32 = mybir.dt.uint32
U16 = mybir.dt.uint16
U8 = mybir.dt.uint8
E4M3 = mybir.dt.float8_e4m3fn_x4
E5M2 = mybir.dt.float8_e5m2_x4
E2M1 = mybir.dt.float4_e2m1fn_x4
SUB = mybir.AluOpType.subtract
MAX = mybir.AluOpType.max
COPY = mybir.ActivationFunctionType.Copy

P = 128
PACK = 4
HALF = J // 2
LIST_COLS = J // 16


def load_scale_rows(engine, plane, scales, r):
    rows = scales[0].bitcast(I32).rearrange("(q r) c -> r q c", r=PACK)
    engine.dma_start(out=plane[r:P:32].bitcast(I32), in_=rows[r])


def load_scale_quadrant(engine, plane, scales, q):
    rows = scales[0, PACK * q : PACK * (q + 1), :].bitcast(I32)
    engine.dma_start(out=plane[32 * q : 32 * (q + 1)].bitcast(I32), in_=rows.unsqueeze(0).to_broadcast([8, PACK, rows.shape[1]]))


def dealt(dst, src, run):
    return (
        dst.rearrange("p (t c i) -> p c t i", t=PACK, i=run),
        src.rearrange("p (c i t) -> p c t i", t=PACK, i=run),
    )


def tile_list_mutual_ahead_skip_plain_kernel(
    tc, xt_words, xt_scales, w_words, w_scales, w2_words, w2_scales, wb_words, wb_scales, ws_words, ws_scales,
    offs, offs2, offs3, offs4, out,
):
    nc = tc.nc
    with ExitStack() as ctx:
        sb = ctx.enter_context(tc.tile_pool(name="sb", bufs=1))
        ps = ctx.enter_context(tc.psum_pool(name="ps", bufs=1))

        def tile(name, shape, dtype, tag=None):
            return sb.tile(shape, dtype, name=name, tag=tag or name, align_bytes=64)

        lists = [sb.tile([P, LIST_COLS], U16, name=f"list{i}") for i in range(4)]
        idx, idx2, idx3, idx4 = lists
        x_words = tile("x_words", [P, T], I32)
        x_scales = tile("x_scales", [P, T], U8)
        w_raw = tile("w_raw", [P, 2 * R], U8)
        w2_raw = tile("w2_raw", [P, 4 * R], U8)
        scale_stage = tile("scale_stage", [P, R], U8)
        scale_stage2 = tile("scale_stage2", [P, R], U8)

        nc.vector.memset(x_scales[:].bitcast(I32), 0)

        nc.sync.dma_start(idx[:], offs)
        for q in range(PACK):
            load_scale_quadrant(nc.scalar if q % 2 else nc.sync, scale_stage[:], w_scales, q)
        nc.scalar.dma_start(out=w_raw[:].bitcast(I32), in_=w_words[0].bitcast(I32))
        nc.sync.dma_start(idx2[:], offs2)
        nc.scalar.dma_start(out=x_words[:], in_=xt_words[0].rearrange("p t b -> p (t b)").bitcast(I32))
        for r in range(PACK):
            load_scale_rows(nc.sync, x_scales[:], xt_scales, r)
        nc.scalar.dma_start(out=w2_raw[:].bitcast(I32), in_=w2_words[0].rearrange("p t b -> p (t b)").bitcast(I32))
        nc.sync.dma_start(idx4[:], offs4)
        nc.sync.dma_start(idx3[:], offs3)

        for q in range(PACK):
            load_scale_quadrant(nc.gpsimd, scale_stage2[:], w2_scales, q)
        x1_words = tile("x1_words", [P, J], U32)
        x1_scales = tile("x1_scales", [P, J], U8)
        x2_scales = tile("x2_scales", [P, J], U8)
        w_codes = tile("w_codes", [P, 2 * R], U8)
        w2_codes = tile("w2_codes", [P, R], U32)
        w_plane = tile("w_plane", [P, R], U8)

        nc.vector.tensor_copy(*dealt(w_plane[:], scale_stage[:], 16))
        nc.vector.tensor_copy(x1_scales[:], x_scales[:].indirect(idx[:]))
        nc.scalar.copy(*dealt(w_codes[:].bitcast(U16), w_raw[:].bitcast(U16), 8))
        nc.vector.tensor_copy(x1_words[:], x_words[:].bitcast(U32).indirect(idx[:]))
        nc.vector.tensor_copy(x2_scales[:], x_scales[:].indirect(idx2[:]))
        x2_words = tile("x2_words", [P, J], U32, tag="x_scales")
        nc.vector.tensor_copy(x2_words[:], x_words[:].bitcast(U32).indirect(idx2[:]))
        nc.scalar.copy(*dealt(w2_codes[:], w2_raw[:].bitcast(U32), 4))
        w2_plane = tile("w2_plane", [P, R], U8, tag="x_words")
        nc.vector.tensor_copy(*dealt(w2_plane[:], scale_stage2[:], 16))

        ws_codes = w2_raw[:, 0 : 2 * N]
        wb_codes = w2_raw[:, 2 * N : 4 * N]
        ws_plane = scale_stage[:, 0:N]
        wb_plane = scale_stage[:, N : 2 * N]
        nc.sync.dma_start(out=ws_codes.bitcast(I32), in_=ws_words[0].bitcast(I32))
        nc.sync.dma_start(out=wb_codes.bitcast(I32), in_=wb_words[0].bitcast(I32))
        for r in range(PACK):
            load_scale_rows(nc.sync, ws_plane, ws_scales, r)
        for r in range(PACK):
            load_scale_rows(nc.sync, wb_plane, wb_scales, r)

        a_sb = tile("a_sb", [P, PACK, J], F32)
        b_sb = [tile(f"b_sb{t}", [P, J], F32) for t in range(PACK)]
        a_picked = tile("a_picked", [P, PACK, J], F32, tag="scale_stage2")
        b_picked = [tile(f"b_picked{h}", [P, PACK, HALF], F32) for h in range(2)]
        d1 = [tile(f"d1_{h}", [P, PACK, HALF], F32) for h in range(2)]
        d2 = tile("d2", [P, PACK, J], F32)

        def half_list(lst, h):
            return lst[:, h * LIST_COLS // 2 : (h + 1) * LIST_COLS // 2]

        for t in range(PACK):
            a_ps = ps.tile([P, J], F32, name=f"a_ps{t}", tag=f"bank_a{t}")
            nc.tensor.matmul_mx(
                out=a_ps[:],
                lhsT=w_codes[:, 2 * P * t : 2 * P * (t + 1)].bitcast(E2M1),
                lhsT_scale=w_plane[:, P * t : P * (t + 1)],
                rhs=x1_words[:].bitcast(E5M2),
                rhs_scale=x1_scales[:],
                start=True,
                stop=True,
            )
            nc.scalar.copy(a_sb[:, t, :], a_ps[:])
        b_ps = []
        for t in range(PACK):
            b_ps.append(ps.tile([P, J], F32, name=f"b_ps{t}", tag=f"bank_b{t}"))
            nc.tensor.matmul_mx(
                out=b_ps[t][:],
                lhsT=w2_codes[:, P * t : P * (t + 1)].bitcast(E4M3),
                lhsT_scale=w2_plane[:, P * t : P * (t + 1)],
                rhs=x2_words[:].bitcast(E5M2),
                rhs_scale=x2_scales[:],
                start=True,
                stop=True,
            )
            nc.scalar.copy(b_sb[t][:], b_ps[t][:])

        for t in range(PACK):
            for h in range(2):
                nc.vector.tensor_copy(
                    a_picked[:, t, h * HALF : (h + 1) * HALF], a_sb[:, t, :].indirect(half_list(idx4, h))
                )
        for h in range(2):
            for t in range(PACK):
                nc.scalar.activation(b_picked[h][:, t, :], b_sb[t][:].indirect(half_list(idx3, h)), COPY)
        for t in range(PACK):
            nc.vector.tensor_tensor(d2[:, t, :], b_ps[t][:], a_picked[:, t, :], SUB)

        y_ps = {}
        for h in range(2):
            cols = slice(h * HALF, (h + 1) * HALF)
            for u in range(2):
                y_ps[(h, u)] = ps.tile([P, HALF], F32, name=f"y_ps{h}{u}", tag=f"bank_b{2 * h + u}")
                nc.tensor.matmul_mx(
                    out=y_ps[(h, u)][:],
                    lhsT=ws_codes[:, 2 * P * u : 2 * P * (u + 1)].bitcast(E2M1),
                    lhsT_scale=ws_plane[:, P * u : P * (u + 1)],
                    rhs=x1_words[:, cols].bitcast(E5M2),
                    rhs_scale=x1_scales[:, cols],
                    start=True,
                    stop=False,
                )

        hid = [tile(f"hid{h}", [P, HALF, PACK], BF16) for h in range(2)]
        hid_codes = [tile(f"hid_codes{h}", [P, HALF], U32) for h in range(2)]
        hid_plane = [tile(f"hid_plane{h}", [P, HALF], U8) for h in range(2)]
        y_sb = [[tile(f"y_sb{h}{u}", [P, HALF], F32) for u in range(2)] for h in range(2)]

        def differ(h):
            nc.vector.tensor_tensor(d1[h][:], a_sb[:, :, h * HALF : (h + 1) * HALF], b_picked[h][:], SUB)

        def larger(h):
            nc.vector.tensor_tensor(
                hid[h][:].rearrange("p (c i) t -> p c t i", i=PACK),
                d1[h][:].rearrange("p t (c i) -> p c t i", i=PACK),
                d2[:, :, h * HALF : (h + 1) * HALF].rearrange("p t (c i) -> p c t i", i=PACK),
                MAX,
            )

        def quantise(h):
            nc.vector.quantize_mx(
                out=hid_codes[h][:].bitcast(E4M3),
                scales=hid_plane[h][:],
                in_=hid[h][:].rearrange("p j t -> p (j t)"),
            )

        def finish(h):
            cols = slice(h * HALF, (h + 1) * HALF)
            for u in range(2):
                nc.tensor.matmul_mx(
                    out=y_ps[(h, u)][:],
                    lhsT=wb_codes[:, 2 * P * u : 2 * P * (u + 1)].bitcast(E2M1),
                    lhsT_scale=wb_plane[:, P * u : P * (u + 1)],
                    rhs=hid_codes[h][:].bitcast(E4M3),
                    rhs_scale=hid_plane[h][:],
                    start=False,
                    stop=True,
                )
            for u in range(2):
                rows = slice(P * u, P * (u + 1))
                if h == 1 and u == 1:
                    nc.vector.tensor_copy(y_sb[h][u][:], y_ps[(h, u)][:])
                else:
                    nc.scalar.copy(y_sb[h][u][:], y_ps[(h, u)][:])
                queue = nc.scalar if (h == 1 and u == 0) else nc.sync
                queue.dma_start(out=out[rows, cols], in_=y_sb[h][u][:])

        differ(0)
        larger(0)
        differ(1)
        quantise(0)
        larger(1)
        finish(0)
        quantise(1)
        finish(1)
